import numpy as np
import ml_dtypes


def mxq(x, axis, fmt="e4m3"):
    dtype, down = {"e4m3": (ml_dtypes.float8_e4m3fn, 7), "e5m2": (ml_dtypes.float8_e5m2, 14)}[fmt]
    v = np.moveaxis(np.asarray(x, np.float32).astype(ml_dtypes.bfloat16).astype(np.float64), axis, -1)
    blocks = v.reshape(v.shape[:-1] + (-1, 32))
    amax = np.abs(blocks).max(-1, keepdims=True)
    byte = np.maximum(np.where(amax > 0, np.frexp(amax)[1] - 1 + 127, 0) - down, 1)
    scale = np.exp2(byte - 127.0)
    codes = (blocks / scale).astype(np.float32).astype(dtype).astype(np.float64)
    return np.moveaxis((codes * scale).reshape(v.shape), -1, axis)


WIDE = False


def mx_kscale(k, group=512):
    if not WIDE:
        return np.ones(k)
    levels = np.array([10, -10, 5, -5, 0])
    if group != 512:
        return np.exp2(np.random.permutation(np.resize(levels, k // group))).repeat(group)
    if k % 512:
        return np.exp2(np.random.permutation(np.resize(levels, k // 32))).repeat(32)
    a = np.empty((k // 512, 16))
    for p in range(k // 512):
        a[p, :8] = np.random.permutation(np.resize(levels, 8))
        for g in range(8):
            far = levels[np.abs(levels - a[p, g]) >= 10]
            a[p, g + 8] = far[np.random.randint(len(far))]
    return np.exp2(a.ravel()).repeat(32)


def f64(x):
    return np.asarray(x).astype(np.float64)


def striped(idx):
    return np.tile(np.asarray(idx).reshape(-1, 16).T, (8, 1)).astype(np.uint16)


def unstriped(offs):
    return offs[:16].T.reshape(-1).astype(np.int64)


H, KV, D, NQ, N = 4, 1, 256, 512, 512


def setup_inputs():
    n = np.random.standard_normal
    s = mx_kscale(D, 0)[:, None]
    u = mx_kscale(N)
    t = np.random.uniform(0.5, 2.0, N) * u
    v = n((KV, N, 128))
    return {
        "qT": (n((H, D, NQ)) * s * (0.70 / np.sqrt(D))).astype(np.float32),
        "kT": (n((KV, D, N)) / s).astype(np.float32),
        "t": t.reshape(N, 1).astype(np.float32),
        "v": (v / t[:, None]).astype(np.float32),
        "gn": np.tile(np.random.uniform(0.5, 2.0, 128), (128, 1)).astype(np.float32),
        "og": n((H, NQ, 128)).astype(np.float32),
    }


def reference(qT, kT, t, v, gn, og):
    a = np.repeat(mxq(f64(kT), 1, "e4m3"), H // KV, 0).transpose(0, 2, 1) @ mxq(f64(qT), 1, "e4m3")
    p = np.maximum(a, 0.0)
    w = p * f64(t)
    y = mxq(w, 1, "e4m3").transpose(0, 2, 1) @ np.repeat(mxq(f64(v), 1, "e4m3"), H // KV, 0)
    y = y / 16.0
    y = y / np.sqrt(np.mean(np.square(y), -1, keepdims=True) + 1e-5) * f64(gn)[:1]
    y = y / (1.0 + np.exp(-f64(og)))
    return y

@@ -1,0 +1,294 @@
+from contextlib import ExitStack
+
+import concourse.mybir as mybir
+
+H, D, NQ, N, E = 4, 256, 512, 512, 128
+FLOPS = 2 * H * N * NQ * D + 2 * H * NQ * N * E
+
+F32 = mybir.dt.float32
+BF16 = mybir.dt.bfloat16
+U32 = mybir.dt.uint32
+U8 = mybir.dt.uint8
+FP8X4 = mybir.dt.float8_e4m3fn_x4
+ACT = mybir.ActivationFunctionType
+ALU = mybir.AluOpType
+
+P = 128
+RT = 64
+UNITS = 8
+GATE_ON_POOL = True
+FINISH = {4: [0], 5: [1, 2, 3], 6: [4], 7: [5], 8: [6]}
+WINDOW = {1: (0, 3), 2: (3, 6), 3: (6, 9), 4: (9, 12), 5: (12, 14), 6: (14, 16)}
+
+
+def tile_rows_a_relu_onorm_gate_kernel(tc, qT, kT, t, v, gn, og, out):
+    nc = tc.nc
+    with ExitStack() as ctx:
+        sb = ctx.enter_context(tc.tile_pool(name="sb", bufs=1))
+        ps = ctx.enter_context(tc.psum_pool(name="ps", bufs=1))
+        ctx.enter_context(tc.manual_schedule())
+
+        k_raw = [sb.tile([P, 4, 256], F32, name="k_raw%d" % i, align_bytes=64) for i in range(2)]
+        k_bf = sb.tile([P, 4, 128, 4], BF16, align_bytes=64)
+        k_codes = sb.tile([P, 512], U32, align_bytes=64)
+        k_scales = sb.tile([P, 512], U8, align_bytes=64)
+        q_spans = [(0, 1), (1, 1), (2, 2), (4, 2), (6, 2)]
+        q_raw = {u0: sb.tile([P, 4, 128 * n], F32, name="q_raw%d" % u0, align_bytes=64) for u0, n in q_spans}
+        q_bf = [sb.tile([P, 128, 4], BF16, name="q_bf%d" % u, align_bytes=64) for u in range(UNITS)]
+        q_codes = [sb.tile([P, 128], U32, name="q_codes%d" % u, align_bytes=64) for u in range(UNITS)]
+        q_scales = [sb.tile([P, 128], U8, name="q_scales%d" % u, align_bytes=64) for u in range(UNITS)]
+        v_raw = sb.tile([P, 4, E], F32, align_bytes=64)
+        v_bf = sb.tile([P, E, 4], BF16, align_bytes=64)
+        v_codes = sb.tile([P, E], U32, align_bytes=64)
+        v_scales = sb.tile([P, E], U8, align_bytes=64)
+        t_sb = sb.tile([P, 4], F32, align_bytes=64)
+        gn_sb = sb.tile([P, E], F32, align_bytes=64)
+        og_sb = sb.tile([P, H, 4, E], F32, align_bytes=64)
+        sig = sb.tile([P, 2, 4, 2, E], F32, align_bytes=64)
+        w_buf = [sb.tile([P, 512], F32, name="w_buf%d" % u, align_bytes=64) for u in range(UNITS)]
+        w_codes = [sb.tile([P, 256], U32, name="w_codes%d" % u, align_bytes=64) for u in range(UNITS)]
+        w_scales = [sb.tile([P, 256], U8, name="w_scales%d" % u, align_bytes=64) for u in range(UNITS)]
+        gate_own = sb.tile([P, 16, E], F32, align_bytes=64)
+        squares = [sb.tile([P, E], BF16, name="squares%d" % i, align_bytes=64) for i in range(2)]
+        ssq = sb.tile([P, 16], F32, align_bytes=64)
+        rstd = sb.tile([P, 16], F32, align_bytes=64)
+        res = [sb.tile([P, 2, E], F32, name="res%d" % u, align_bytes=64) for u in range(UNITS)]
+        s_ps = [[ps.tile([P, 4, 128], F32, name="s_ps%d%d" % (hh, i)) for i in range(2)] for hh in range(2)]
+        y_ps = [ps.tile([P, 4, E], F32, name="y_ps%d" % i) for i in range(4)]
+
+        sig_n = sig[:].rearrange("p g c h e -> p (g c h) e")
+        gate_at = {}
+
+        def load_q(u0, n):
+            g, c = divmod(u0, 4)
+            src = qT[2 * g : 2 * g + 2].rearrange("h (p j) q -> (h p) j q", j=4)
+            nc.sync.dma_start(out=q_raw[u0][:], in_=src[:, :, 128 * c : 128 * (c + n)])
+
+        def load_og(eng, h0, nh, c0, nchunk):
+            src = og[h0 : h0 + nh].rearrange("h (c p) e -> p h c e", p=P)
+            if nh == 1:
+                eng.dma_start(out=og_sb[:, h0, c0 : c0 + nchunk, :], in_=src[:, 0, c0 : c0 + nchunk, :])
+            else:
+                eng.dma_start(
+                    out=og_sb[:, h0 : h0 + nh].rearrange("p h c e -> p (h c) e"),
+                    in_=og[h0 : h0 + nh].rearrange("h (c p) e -> p (h c) e", p=P),
+                )
+
+        def sigmoid(h, c0, nchunk):
+            g, hh = divmod(h, 2)
+            nc.scalar.activation(
+                out=sig[:, g, c0 : c0 + nchunk, hh, :], in_=og_sb[:, h, c0 : c0 + nchunk, :], func=ACT.Sigmoid
+            )
+
+        def cast_k(half):
+            dst = k_bf[:, :, 64 * half : 64 * half + 64, :].rearrange("p r s j -> p s r j")
+            src = k_raw[half][:].rearrange("p j (s r) -> p s r j", r=4)
+            nc.vector.tensor_copy(out=dst, in_=src)
+
+        def interleave(eng_copy, dst, src):
+            eng_copy(
+                out=dst.rearrange("p (c i) j -> p c j i", i=4),
+                in_=src.rearrange("p j (c i) -> p c j i", i=4),
+            )
+
+        def cast_q(u):
+            u0 = max(s for s, n in q_spans if s <= u)
+            interleave(nc.scalar.copy, q_bf[u][:], q_raw[u0][:, :, 128 * (u - u0) : 128 * (u - u0 + 1)])
+
+        def quant_q(u):
+            nc.vector.quantize_mx(
+                out=q_codes[u][:].bitcast(FP8X4), scales=q_scales[u][:], in_=q_bf[u][:].rearrange("p q j -> p (q j)")
+            )
+
+        def scores(u):
+            for r in range(4):
+                for hh in range(2):
+                    rows = slice(RT * hh, RT * hh + RT)
+                    cols = slice(128 * r, 128 * r + 128)
+                    nc.tensor.matmul_mx(
+                        out=s_ps[hh][u % 2][:, r, :],
+                        lhsT=k_codes[rows, cols].bitcast(FP8X4),
+                        lhsT_scale=k_scales[rows, cols],
+                        rhs=q_codes[u][rows, :].bitcast(FP8X4),
+                        rhs_scale=q_scales[u][rows, :],
+                        start=True,
+                        stop=True,
+                    )
+
+        def w_bf(u):
+            return w_buf[u][:].bitcast(BF16)
+
+        def weigh(u, hh):
+            nc.vector.scalar_tensor_tensor(
+                out=w_bf(u)[:, 512 * hh : 512 * hh + 512].rearrange("p (q r) -> p q r", r=4),
+                in0=s_ps[hh][u % 2][:].rearrange("p r q -> p q r"),
+                scalar=0.0,
+                in1=t_sb[:].unsqueeze(1).broadcast_to([P, 128, 4]),
+                op0=ALU.max,
+                op1=ALU.mult,
+            )
+
+        def quant_w(u, h0, nh):
+            cols = slice(128 * h0, 128 * (h0 + nh))
+            nc.vector.quantize_mx(
+                out=w_codes[u][:, cols].bitcast(FP8X4),
+                scales=w_scales[u][:, cols],
+                in_=w_bf(u)[:, 512 * h0 : 512 * (h0 + nh)],
+            )
+
+        def y_of(u, hh):
+            return y_ps[u // 2][:, 2 * (u % 2) + hh, :]
+
+        def values(u, hh):
+            cols = slice(128 * hh, 128 * hh + 128)
+            nc.tensor.matmul_mx(
+                out=y_of(u, hh),
+                lhsT=w_codes[u][:, cols].bitcast(FP8X4),
+                lhsT_scale=w_scales[u][:, cols],
+                rhs=v_codes[:].bitcast(FP8X4),
+                rhs_scale=v_scales[:],
+                start=True,
+                stop=True,
+            )
+
+        def sum_squares(u, hh):
+            n = 2 * u + hh
+            nc.scalar.activation(out=squares[hh][:], in_=y_of(u, hh), func=ACT.Square, accum_out=ssq[:, n : n + 1])
+
+        def inv_rms(n0, n1):
+            nc.scalar.activation(
+                out=rstd[:, n0:n1], in_=ssq[:, n0:n1], func=ACT.Abs_reciprocal_sqrt, scale=1.0 / E, bias=256.0 * 1e-5
+            )
+
+        def gates(n0, n1, u):
+            cnt = n1 - n0
+            if GATE_ON_POOL:
+                dst = w_buf[u][:, 0 : cnt * E].rearrange("p (n e) -> p n e", e=E)
+                eng = nc.gpsimd
+            else:
+                dst = gate_own[:, n0:n1, :]
+                eng = nc.vector
+            for n in range(n0, n1):
+                gate_at[n] = dst[:, n - n0, :]
+            eng.tensor_tensor(
+                out=dst, in0=sig_n[:, n0:n1, :], in1=gn_sb[:].unsqueeze(1).broadcast_to([P, cnt, E]), op=ALU.mult
+            )
+
+        def finish(u, hh):
+            n = 2 * u + hh
+            nc.vector.scalar_tensor_tensor(
+                out=res[u][:, hh, :],
+                in0=y_of(u, hh),
+                scalar=rstd[:, n : n + 1],
+                in1=gate_at[n],
+                op0=ALU.mult,
+                op1=ALU.mult,
+            )
+
+        def store(u, h0, nh):
+            g, c = divmod(u, 4)
+            dst = out[2 * g + h0 : 2 * g + h0 + nh, 128 * c : 128 * c + 128, :].rearrange("h p e -> p h e")
+            nc.sync.dma_start(out=dst, in_=res[u][:, h0 : h0 + nh, :])
+
+        k_src = kT[0].rearrange("(p j) n -> p j n", j=4)
+        load_og(nc.gpsimd, 0, 1, 0, 1)
+        nc.gpsimd.dma_start(out=t_sb[:], in_=t.rearrange("(p j) o -> p (j o)", j=4))
+        nc.gpsimd.dma_start(out=gn_sb[:], in_=gn)
+        for half in range(2):
+            cols = slice(256 * half, 256 * half + 256)
+            nc.sync.dma_start(out=k_raw[half][0:RT], in_=k_src[:, :, cols])
+            nc.scalar.dma_start(out=k_raw[half][RT:P], in_=k_src[:, :, cols])
+        load_q(0, 1)
+        load_q(1, 1)
+        load_q(2, 2)
+        nc.sync.dma_start(out=v_raw[:], in_=v[0].rearrange("(p j) e -> p j e", j=4))
+        load_og(nc.sync, 0, 1, 1, 3)
+        load_og(nc.sync, 1, 1, 0, 4)
+        load_q(4, 2)
+        load_og(nc.sync, 2, 2, 0, 4)
+        load_q(6, 2)
+
+        sigmoid(0, 0, 1)
+        cast_k(0)
+        cast_k(1)
+        cast_q(0)
+        for rr in range(2):
+            cols = slice(256 * rr, 256 * rr + 256)
+            nc.vector.quantize_mx(
+                out=k_codes[:, cols].bitcast(FP8X4),
+                scales=k_scales[:, cols],
+                in_=k_bf[:, 2 * rr : 2 * rr + 2].rearrange("p r s j -> p (r s j)"),
+            )
+        quant_q(0)
+        scores(0)
+        cast_q(1)
+        quant_q(1)
+        scores(1)
+        cast_q(2)
+        cast_q(3)
+        interleave(nc.scalar.copy, v_bf[:], v_raw[:])
+        sigmoid(0, 1, 3)
+        sigmoid(1, 0, 4)
+
+        for u in range(UNITS):
+            last = u == UNITS - 1
+            weigh(u, 0)
+            weigh(u, 1)
+            if last:
+                quant_w(u, 0, 1)
+                values(u, 0)
+                sum_squares(u, 0)
+                inv_rms(2 * u, 2 * u + 1)
+            for f in FINISH.get(u, []):
+                finish(f, 0)
+                finish(f, 1)
+                store(f, 0, 2)
+            if last:
+                quant_w(u, 1, 1)
+                values(u, 1)
+                sum_squares(u, 1)
+                inv_rms(2 * u + 1, 2 * u + 2)
+                break
+            if u == 1:
+                nc.vector.quantize_mx(
+                    out=v_codes[:].bitcast(FP8X4), scales=v_scales[:], in_=v_bf[:].rearrange("p e j -> p (e j)")
+                )
+                values(0, 0)
+                values(0, 1)
+            if u + 2 < UNITS:
+                quant_q(u + 2)
+                scores(u + 2)
+            quant_w(u, 0, 2)
+            if u >= 1:
+                values(u, 0)
+                values(u, 1)
+            if u == 0:
+                cast_q(4)
+            if u == 1:
+                cast_q(5)
+                sigmoid(2, 0, 4)
+                sigmoid(3, 0, 4)
+                sum_squares(0, 0)
+                sum_squares(0, 1)
+                inv_rms(0, 2)
+            if u == 2:
+                cast_q(6)
+                for f in (1, 2):
+                    sum_squares(f, 0)
+                    sum_squares(f, 1)
+                    inv_rms(2 * f, 2 * f + 2)
+            if u == 3:
+                cast_q(7)
+            if u >= 3:
+                sum_squares(u, 0)
+                sum_squares(u, 1)
+                inv_rms(2 * u, 2 * u + 2)
+            if u in WINDOW:
+                gates(WINDOW[u][0], WINDOW[u][1], u)
+        for f in FINISH[UNITS]:
+            finish(f, 0)
+            finish(f, 1)
+            store(f, 0, 2)
+        for hh in range(2):
+            finish(UNITS - 1, hh)
+            store(UNITS - 1, hh, 1)

@@ -16,9 +16,9 @@ ALU = mybir.AluOpType
 P = 128
 RT = 64
 UNITS = 8
-GATE_ON_POOL = True
+GATE_ON_POOL = False
 FINISH = {4: [0], 5: [1, 2, 3], 6: [4], 7: [5], 8: [6]}
-WINDOW = {1: (0, 3), 2: (3, 6), 3: (6, 9), 4: (9, 12), 5: (12, 14), 6: (14, 16)}
+WINDOW = {1: (0, 4), 3: (4, 8), 5: (8, 12), 6: (12, 16)}
 
 
 def tile_rows_a_relu_onorm_gate_kernel(tc, qT, kT, t, v, gn, og, out):
@@ -34,9 +34,9 @@ def tile_rows_a_relu_onorm_gate_kernel(tc, qT, kT, t, v, gn, og, out):
         k_scales = sb.tile([P, 512], U8, align_bytes=64)
         q_spans = [(0, 1), (1, 1), (2, 2), (4, 2), (6, 2)]
         q_raw = {u0: sb.tile([P, 4, 128 * n], F32, name="q_raw%d" % u0, align_bytes=64) for u0, n in q_spans}
-        q_bf = [sb.tile([P, 128, 4], BF16, name="q_bf%d" % u, align_bytes=64) for u in range(UNITS)]
-        q_codes = [sb.tile([P, 128], U32, name="q_codes%d" % u, align_bytes=64) for u in range(UNITS)]
-        q_scales = [sb.tile([P, 128], U8, name="q_scales%d" % u, align_bytes=64) for u in range(UNITS)]
+        q_bf = {u0: sb.tile([P, 128 * n, 4], BF16, name="q_bf%d" % u0, align_bytes=64) for u0, n in q_spans}
+        q_codes = sb.tile([P, 128 * UNITS], U32, align_bytes=64)
+        q_scales = sb.tile([P, 128 * UNITS], U8, align_bytes=64)
         v_raw = sb.tile([P, 4, E], F32, align_bytes=64)
         v_bf = sb.tile([P, E, 4], BF16, align_bytes=64)
         v_codes = sb.tile([P, E], U32, align_bytes=64)
@@ -91,13 +91,13 @@ def tile_rows_a_relu_onorm_gate_kernel(tc, qT, kT, t, v, gn, og, out):
                 in_=src.rearrange("p j (c i) -> p c j i", i=4),
             )
 
-        def cast_q(u):
-            u0 = max(s for s, n in q_spans if s <= u)
-            interleave(nc.scalar.copy, q_bf[u][:], q_raw[u0][:, :, 128 * (u - u0) : 128 * (u - u0 + 1)])
+        def cast_q(u0):
+            interleave(nc.scalar.copy, q_bf[u0][:], q_raw[u0][:])
 
-        def quant_q(u):
+        def quant_q(u0):
+            cols = slice(128 * u0, 128 * (u0 + dict(q_spans)[u0]))
             nc.vector.quantize_mx(
-                out=q_codes[u][:].bitcast(FP8X4), scales=q_scales[u][:], in_=q_bf[u][:].rearrange("p q j -> p (q j)")
+                out=q_codes[:, cols].bitcast(FP8X4), scales=q_scales[:, cols], in_=q_bf[u0][:].rearrange("p q j -> p (q j)")
             )
 
         def scores(u):
@@ -109,8 +109,8 @@ def tile_rows_a_relu_onorm_gate_kernel(tc, qT, kT, t, v, gn, og, out):
                         out=s_ps[hh][u % 2][:, r, :],
                         lhsT=k_codes[rows, cols].bitcast(FP8X4),
                         lhsT_scale=k_scales[rows, cols],
-                        rhs=q_codes[u][rows, :].bitcast(FP8X4),
-                        rhs_scale=q_scales[u][rows, :],
+                        rhs=q_codes[rows, 128 * u : 128 * u + 128].bitcast(FP8X4),
+                        rhs_scale=q_scales[rows, 128 * u : 128 * u + 128],
                         start=True,
                         stop=True,
                     )
@@ -137,7 +137,7 @@ def tile_rows_a_relu_onorm_gate_kernel(tc, qT, kT, t, v, gn, og, out):
             )
 
         def y_of(u, hh):
-            return y_ps[u // 2][:, 2 * (u % 2) + hh, :]
+            return y_ps[2 * (u % 2) + hh][:, u // 2, :]
 
         def values(u, hh):
             cols = slice(128 * hh, 128 * hh + 128)
@@ -191,17 +191,17 @@ def tile_rows_a_relu_onorm_gate_kernel(tc, qT, kT, t, v, gn, og, out):
             nc.sync.dma_start(out=dst, in_=res[u][:, h0 : h0 + nh, :])
 
         k_src = kT[0].rearrange("(p j) n -> p j n", j=4)
-        load_og(nc.gpsimd, 0, 1, 0, 1)
-        nc.gpsimd.dma_start(out=t_sb[:], in_=t.rearrange("(p j) o -> p (j o)", j=4))
-        nc.gpsimd.dma_start(out=gn_sb[:], in_=gn)
+        load_og(nc.scalar, 0, 1, 0, 1)
         for half in range(2):
             cols = slice(256 * half, 256 * half + 256)
             nc.sync.dma_start(out=k_raw[half][0:RT], in_=k_src[:, :, cols])
             nc.scalar.dma_start(out=k_raw[half][RT:P], in_=k_src[:, :, cols])
+        nc.scalar.dma_start(out=t_sb[:], in_=t.rearrange("(p j) o -> p (j o)", j=4))
         load_q(0, 1)
         load_q(1, 1)
         load_q(2, 2)
         nc.sync.dma_start(out=v_raw[:], in_=v[0].rearrange("(p j) e -> p j e", j=4))
+        nc.sync.dma_start(out=gn_sb[:], in_=gn)
         load_og(nc.sync, 0, 1, 1, 3)
         load_og(nc.sync, 1, 1, 0, 4)
         load_q(4, 2)
@@ -225,7 +225,6 @@ def tile_rows_a_relu_onorm_gate_kernel(tc, qT, kT, t, v, gn, og, out):
         quant_q(1)
         scores(1)
         cast_q(2)
-        cast_q(3)
         interleave(nc.scalar.copy, v_bf[:], v_raw[:])
         sigmoid(0, 1, 3)
         sigmoid(1, 0, 4)
@@ -239,6 +238,8 @@ def tile_rows_a_relu_onorm_gate_kernel(tc, qT, kT, t, v, gn, og, out):
                 values(u, 0)
                 sum_squares(u, 0)
                 inv_rms(2 * u, 2 * u + 1)
+            if u in WINDOW:
+                gates(WINDOW[u][0], WINDOW[u][1], u)
             for f in FINISH.get(u, []):
                 finish(f, 0)
                 finish(f, 1)
@@ -256,7 +257,8 @@ def tile_rows_a_relu_onorm_gate_kernel(tc, qT, kT, t, v, gn, og, out):
                 values(0, 0)
                 values(0, 1)
             if u + 2 < UNITS:
-                quant_q(u + 2)
+                if u % 2 == 0:
+                    quant_q(u + 2)
                 scores(u + 2)
             quant_w(u, 0, 2)
             if u >= 1:
@@ -265,7 +267,6 @@ def tile_rows_a_relu_onorm_gate_kernel(tc, qT, kT, t, v, gn, og, out):
             if u == 0:
                 cast_q(4)
             if u == 1:
-                cast_q(5)
                 sigmoid(2, 0, 4)
                 sigmoid(3, 0, 4)
                 sum_squares(0, 0)
@@ -277,14 +278,10 @@ def tile_rows_a_relu_onorm_gate_kernel(tc, qT, kT, t, v, gn, og, out):
                     sum_squares(f, 0)
                     sum_squares(f, 1)
                     inv_rms(2 * f, 2 * f + 2)
-            if u == 3:
-                cast_q(7)
             if u >= 3:
                 sum_squares(u, 0)
                 sum_squares(u, 1)
                 inv_rms(2 * u, 2 * u + 2)
-            if u in WINDOW:
-                gates(WINDOW[u][0], WINDOW[u][1], u)
         for f in FINISH[UNITS]:
             finish(f, 0)
             finish(f, 1)

@@ -16,9 +16,10 @@ ALU = mybir.AluOpType
 P = 128
 RT = 64
 UNITS = 8
-GATE_ON_POOL = False
+GATE_ON_POOL = True
 FINISH = {4: [0], 5: [1, 2, 3], 6: [4], 7: [5], 8: [6]}
-WINDOW = {1: (0, 4), 3: (4, 8), 5: (8, 12), 6: (12, 16)}
+PAIRED = [1]
+WINDOW = {1: (0, 3), 2: (3, 6), 3: (6, 9), 4: (9, 12), 5: (12, 14), 6: (14, 16)}
 
 
 def tile_rows_a_relu_onorm_gate_kernel(tc, qT, kT, t, v, gn, og, out):
@@ -42,6 +43,11 @@ def tile_rows_a_relu_onorm_gate_kernel(tc, qT, kT, t, v, gn, og, out):
         v_codes = sb.tile([P, E], U32, align_bytes=64)
         v_scales = sb.tile([P, E], U8, align_bytes=64)
         t_sb = sb.tile([P, 4], F32, align_bytes=64)
+        t_rep = sb.tile([P, 128, 4], F32, align_bytes=64)
+        t_pair = sb.tile([P, 64, 4, 2], F32, align_bytes=64)
+        t_two = sb.tile([P, 4], F32, align_bytes=64)
+        t_sign = sb.tile([P, 4], F32, align_bytes=64)
+        v_sgn = sb.tile([P, 4, E], F32, align_bytes=64)
         gn_sb = sb.tile([P, E], F32, align_bytes=64)
         og_sb = sb.tile([P, H, 4, E], F32, align_bytes=64)
         sig = sb.tile([P, 2, 4, 2, E], F32, align_bytes=64)
@@ -102,7 +108,7 @@ def tile_rows_a_relu_onorm_gate_kernel(tc, qT, kT, t, v, gn, og, out):
 
         def scores(u):
             for r in range(4):
-                for hh in range(2):
+                for hh in (1, 0):
                     rows = slice(RT * hh, RT * hh + RT)
                     cols = slice(128 * r, 128 * r + 128)
                     nc.tensor.matmul_mx(
@@ -119,13 +125,28 @@ def tile_rows_a_relu_onorm_gate_kernel(tc, qT, kT, t, v, gn, og, out):
             return w_buf[u][:].bitcast(BF16)
 
         def weigh(u, hh):
-            nc.vector.scalar_tensor_tensor(
-                out=w_bf(u)[:, 512 * hh : 512 * hh + 512].rearrange("p (q r) -> p q r", r=4),
-                in0=s_ps[hh][u % 2][:].rearrange("p r q -> p q r"),
-                scalar=0.0,
-                in1=t_sb[:].unsqueeze(1).broadcast_to([P, 128, 4]),
-                op0=ALU.max,
-                op1=ALU.mult,
+            dst = w_bf(u)[:, 512 * hh : 512 * hh + 512]
+            if hh in PAIRED:
+                nc.vector.tensor_tensor(
+                    out=dst.rearrange("p (c i r) -> p c r i", r=4, i=2),
+                    in0=s_ps[hh][u % 2][:].rearrange("p r (c i) -> p c r i", i=2),
+                    in1=t_pair[:],
+                    op=ALU.mult,
+                )
+            else:
+                nc.vector.scalar_tensor_tensor(
+                    out=dst.rearrange("p (q r) -> p q r", r=4),
+                    in0=s_ps[hh][u % 2][:].rearrange("p r q -> p q r"),
+                    scalar=0.0,
+                    in1=t_rep[:],
+                    op0=ALU.max,
+                    op1=ALU.mult,
+                )
+
+        def relu(u):
+            lo, hi = 512 * min(PAIRED), 512 * max(PAIRED) + 512
+            nc.vector.tensor_scalar(
+                out=w_bf(u)[:, lo:hi], in0=w_bf(u)[:, lo:hi], scalar1=0.0, scalar2=None, op0=ALU.max
             )
 
         def quant_w(u, h0, nh):
@@ -191,12 +212,12 @@ def tile_rows_a_relu_onorm_gate_kernel(tc, qT, kT, t, v, gn, og, out):
             nc.sync.dma_start(out=dst, in_=res[u][:, h0 : h0 + nh, :])
 
         k_src = kT[0].rearrange("(p j) n -> p j n", j=4)
+        nc.scalar.dma_start(out=t_sb[:], in_=t.rearrange("(p j) o -> p (j o)", j=4))
         load_og(nc.scalar, 0, 1, 0, 1)
         for half in range(2):
             cols = slice(256 * half, 256 * half + 256)
             nc.sync.dma_start(out=k_raw[half][0:RT], in_=k_src[:, :, cols])
             nc.scalar.dma_start(out=k_raw[half][RT:P], in_=k_src[:, :, cols])
-        nc.scalar.dma_start(out=t_sb[:], in_=t.rearrange("(p j) o -> p (j o)", j=4))
         load_q(0, 1)
         load_q(1, 1)
         load_q(2, 2)
@@ -209,6 +230,12 @@ def tile_rows_a_relu_onorm_gate_kernel(tc, qT, kT, t, v, gn, og, out):
         load_q(6, 2)
 
         sigmoid(0, 0, 1)
+        nc.gpsimd.tensor_scalar(out=t_two[:], in0=t_sb[:], scalar1=0.0, scalar2=2.0, op0=ALU.is_ge, op1=ALU.mult)
+        nc.gpsimd.tensor_scalar(out=t_sign[:], in0=t_two[:], scalar1=1.0, scalar2=-1.0, op0=ALU.mult, op1=ALU.add)
+        nc.scalar.activation(
+            out=t_pair[:], in_=t_sb[:].unsqueeze(1).unsqueeze(3).broadcast_to([P, 64, 4, 2]), func=ACT.Abs
+        )
+        nc.scalar.activation(out=t_rep[:], in_=t_sb[:].unsqueeze(1).broadcast_to([P, 128, 4]), func=ACT.Abs)
         cast_k(0)
         cast_k(1)
         cast_q(0)
@@ -225,31 +252,33 @@ def tile_rows_a_relu_onorm_gate_kernel(tc, qT, kT, t, v, gn, og, out):
         quant_q(1)
         scores(1)
         cast_q(2)
-        interleave(nc.scalar.copy, v_bf[:], v_raw[:])
+        for j in range(4):
+            nc.scalar.activation(out=v_sgn[:, j, :], in_=v_raw[:, j, :], func=ACT.Copy, scale=t_sign[:, j : j + 1])
+        interleave(nc.scalar.copy, v_bf[:], v_sgn[:])
         sigmoid(0, 1, 3)
         sigmoid(1, 0, 4)
 
         for u in range(UNITS):
             last = u == UNITS - 1
-            weigh(u, 0)
             weigh(u, 1)
+            weigh(u, 0)
             if last:
+                relu(u)
                 quant_w(u, 0, 1)
                 values(u, 0)
                 sum_squares(u, 0)
                 inv_rms(2 * u, 2 * u + 1)
-            if u in WINDOW:
-                gates(WINDOW[u][0], WINDOW[u][1], u)
+                quant_w(u, 1, 1)
+                values(u, 1)
+                sum_squares(u, 1)
+                inv_rms(2 * u + 1, 2 * u + 2)
             for f in FINISH.get(u, []):
                 finish(f, 0)
                 finish(f, 1)
                 store(f, 0, 2)
             if last:
-                quant_w(u, 1, 1)
-                values(u, 1)
-                sum_squares(u, 1)
-                inv_rms(2 * u + 1, 2 * u + 2)
                 break
+            relu(u)
             if u == 1:
                 nc.vector.quantize_mx(
                     out=v_codes[:].bitcast(FP8X4), scales=v_scales[:], in_=v_bf[:].rearrange("p e j -> p (e j)")
@@ -260,7 +289,8 @@ def tile_rows_a_relu_onorm_gate_kernel(tc, qT, kT, t, v, gn, og, out):
                 if u % 2 == 0:
                     quant_q(u + 2)
                 scores(u + 2)
-            quant_w(u, 0, 2)
+            quant_w(u, 0, 1)
+            quant_w(u, 1, 1)
             if u >= 1:
                 values(u, 0)
                 values(u, 1)
@@ -282,6 +312,8 @@ def tile_rows_a_relu_onorm_gate_kernel(tc, qT, kT, t, v, gn, og, out):
                 sum_squares(u, 0)
                 sum_squares(u, 1)
                 inv_rms(2 * u, 2 * u + 2)
+            if u in WINDOW:
+                gates(WINDOW[u][0], WINDOW[u][1], u)
         for f in FINISH[UNITS]:
             finish(f, 0)
             finish(f, 1)

@@ -14,12 +14,20 @@ ACT = mybir.ActivationFunctionType
 ALU = mybir.AluOpType
 
 P = 128
-RT = 64
-UNITS = 8
-GATE_ON_POOL = True
-FINISH = {4: [0], 5: [1, 2, 3], 6: [4], 7: [5], 8: [6]}
-PAIRED = [1]
-WINDOW = {1: (0, 3), 2: (3, 6), 3: (6, 9), 4: (9, 12), 5: (12, 14), 6: (14, 16)}
+PACK = 4
+ROWS = D // PACK
+QU = 128
+UNITS = H // 2 * NQ // QU
+HALF = N // 2
+SH = HALF // PACK
+EPS = 1e-5
+Y_DIV = 16.0
+
+Q_LOADS = {0: 1, 1: 1, 2: 2, 4: 2, 6: 2}
+Y_PLACE = [(1, 0), (1, 1), (0, 0), (1, 2), (0, 1), (0, 2), (0, 3), (1, 3)]
+GATE_BATCH = [(0, 1), (1, 3), (3, 5), (5, 7), (7, 11), (11, 14), (14, 16)]
+FINISH_IN_STEP = {5: [0, 1], 6: [3]}
+SQUARES_IN_STEP = {5: ([2, 4, 3], (4, 10)), 6: ([5], (10, 12))}
 
 
 def tile_rows_a_relu_onorm_gate_kernel(tc, qT, kT, t, v, gn, og, out):
@@ -29,139 +37,135 @@ def tile_rows_a_relu_onorm_gate_kernel(tc, qT, kT, t, v, gn, og, out):
         ps = ctx.enter_context(tc.psum_pool(name="ps", bufs=1))
         ctx.enter_context(tc.manual_schedule())
 
-        k_raw = [sb.tile([P, 4, 256], F32, name="k_raw%d" % i, align_bytes=64) for i in range(2)]
-        k_bf = sb.tile([P, 4, 128, 4], BF16, align_bytes=64)
-        k_codes = sb.tile([P, 512], U32, align_bytes=64)
-        k_scales = sb.tile([P, 512], U8, align_bytes=64)
-        q_spans = [(0, 1), (1, 1), (2, 2), (4, 2), (6, 2)]
-        q_raw = {u0: sb.tile([P, 4, 128 * n], F32, name="q_raw%d" % u0, align_bytes=64) for u0, n in q_spans}
-        q_bf = {u0: sb.tile([P, 128 * n, 4], BF16, name="q_bf%d" % u0, align_bytes=64) for u0, n in q_spans}
-        q_codes = sb.tile([P, 128 * UNITS], U32, align_bytes=64)
-        q_scales = sb.tile([P, 128 * UNITS], U8, align_bytes=64)
-        v_raw = sb.tile([P, 4, E], F32, align_bytes=64)
-        v_bf = sb.tile([P, E, 4], BF16, align_bytes=64)
-        v_codes = sb.tile([P, E], U32, align_bytes=64)
-        v_scales = sb.tile([P, E], U8, align_bytes=64)
-        t_sb = sb.tile([P, 4], F32, align_bytes=64)
-        t_rep = sb.tile([P, 128, 4], F32, align_bytes=64)
-        t_pair = sb.tile([P, 64, 4, 2], F32, align_bytes=64)
-        t_two = sb.tile([P, 4], F32, align_bytes=64)
-        t_sign = sb.tile([P, 4], F32, align_bytes=64)
-        v_sgn = sb.tile([P, 4, E], F32, align_bytes=64)
-        gn_sb = sb.tile([P, E], F32, align_bytes=64)
-        og_sb = sb.tile([P, H, 4, E], F32, align_bytes=64)
-        sig = sb.tile([P, 2, 4, 2, E], F32, align_bytes=64)
-        w_buf = [sb.tile([P, 512], F32, name="w_buf%d" % u, align_bytes=64) for u in range(UNITS)]
-        w_codes = [sb.tile([P, 256], U32, name="w_codes%d" % u, align_bytes=64) for u in range(UNITS)]
-        w_scales = [sb.tile([P, 256], U8, name="w_scales%d" % u, align_bytes=64) for u in range(UNITS)]
-        gate_own = sb.tile([P, 16, E], F32, align_bytes=64)
-        squares = [sb.tile([P, E], BF16, name="squares%d" % i, align_bytes=64) for i in range(2)]
-        ssq = sb.tile([P, 16], F32, align_bytes=64)
-        rstd = sb.tile([P, 16], F32, align_bytes=64)
-        res = [sb.tile([P, 2, E], F32, name="res%d" % u, align_bytes=64) for u in range(UNITS)]
-        s_ps = [[ps.tile([P, 4, 128], F32, name="s_ps%d%d" % (hh, i)) for i in range(2)] for hh in range(2)]
+        def sbuf(name, shape, dtype):
+            return sb.tile([P] + shape, dtype, name=name, align_bytes=64)
+
+        k_raw = [sbuf("k_raw%d" % half, [PACK, HALF], F32) for half in range(2)]
+        k_bf = sbuf("k_bf", [PACK, P, PACK], BF16)
+        k_codes = sbuf("k_codes", [N], U32)
+        k_scales = sbuf("k_scales", [N], U8)
+        q_raw = {u0: sbuf("q_raw%d" % u0, [PACK, QU * n], F32) for u0, n in Q_LOADS.items()}
+        q_bf = [sbuf("q_bf%d" % u, [QU, PACK], BF16) for u in range(UNITS)]
+        q_codes = [sbuf("q_codes%d" % u, [QU], U32) for u in range(UNITS)]
+        q_scales = [sbuf("q_scales%d" % u, [QU], U8) for u in range(UNITS)]
+        v_raw = sbuf("v_raw", [PACK, E], F32)
+        v_bf = sbuf("v_bf", [E, PACK], BF16)
+        v_codes = sbuf("v_codes", [E], U32)
+        v_scales = sbuf("v_scales", [E], U8)
+        t_sb = sbuf("t_sb", [PACK], F32)
+        gn_sb = sbuf("gn_sb", [E], F32)
+        og_sb = sbuf("og_sb", [H, UNITS // 2, E], F32)
+        sig = sbuf("sig", [UNITS, 2, E], F32)
+        w_buf = [sbuf("w_buf%d" % u, [QU * PACK], F32) for u in range(UNITS)]
+        w_codes = [sbuf("w_codes%d" % u, [2 * QU], U32) for u in range(UNITS)]
+        w_scales = [sbuf("w_scales%d" % u, [2 * QU], U8) for u in range(UNITS)]
+        squares = [sbuf("squares%d" % hh, [E], BF16) for hh in range(2)]
+        ssq = sbuf("ssq", [2 * UNITS], F32)
+        inv_norm = sbuf("inv_norm", [2 * UNITS], F32)
+        res = [sbuf("res%d" % c, [2, 2, E], F32) for c in range(UNITS // 2)]
+        s_ps = [[ps.tile([P, PACK, QU], F32, name="s_ps%d%d" % (hh, i)) for i in range(2)] for hh in range(2)]
         y_ps = [ps.tile([P, 4, E], F32, name="y_ps%d" % i) for i in range(4)]
+        gate_of = {}
+        queue_of_row_tile = (nc.sync, nc.scalar)
 
-        sig_n = sig[:].rearrange("p g c h e -> p (g c h) e")
-        gate_at = {}
+        def row_tile(hh):
+            return slice(ROWS * hh, ROWS * hh + ROWS)
 
-        def load_q(u0, n):
+        def couple_rows(dram, u):
+            g, c = divmod(u, 4)
+            rows = dram[2 * g : 2 * g + 2, QU * c : QU * (c + 2), :]
+            return rows.rearrange("h (m c) e -> m h (c e)", c=2)
+
+        def load_q(u0):
             g, c = divmod(u0, 4)
-            src = qT[2 * g : 2 * g + 2].rearrange("h (p j) q -> (h p) j q", j=4)
-            nc.sync.dma_start(out=q_raw[u0][:], in_=src[:, :, 128 * c : 128 * (c + n)])
+            src = qT[2 * g : 2 * g + 2].rearrange("h (p j) q -> (h p) j q", j=PACK)
+            nc.sync.dma_start(out=q_raw[u0][:], in_=src[:, :, QU * c : QU * (c + Q_LOADS[u0])])
 
-        def load_og(eng, h0, nh, c0, nchunk):
-            src = og[h0 : h0 + nh].rearrange("h (c p) e -> p h c e", p=P)
-            if nh == 1:
-                eng.dma_start(out=og_sb[:, h0, c0 : c0 + nchunk, :], in_=src[:, 0, c0 : c0 + nchunk, :])
-            else:
-                eng.dma_start(
-                    out=og_sb[:, h0 : h0 + nh].rearrange("p h c e -> p (h c) e"),
-                    in_=og[h0 : h0 + nh].rearrange("h (c p) e -> p (h c) e", p=P),
-                )
+        def load_og(eng, h, u0, u1):
+            src = og[h].rearrange("(c m) e -> m c e", m=P)
+            eng.dma_start(out=og_sb[:, h, u0:u1, :], in_=src[:, u0:u1, :])
 
-        def sigmoid(h, c0, nchunk):
-            g, hh = divmod(h, 2)
-            nc.scalar.activation(
-                out=sig[:, g, c0 : c0 + nchunk, hh, :], in_=og_sb[:, h, c0 : c0 + nchunk, :], func=ACT.Sigmoid
-            )
+        def load_og_couple(u):
+            g, c = divmod(u, 4)
+            dst = og_sb[:, 2 * g : 2 * g + 2, c : c + 2, :].rearrange("m h c e -> m h (c e)")
+            nc.sync.dma_start(out=dst, in_=couple_rows(og, u))
 
-        def cast_k(half):
-            dst = k_bf[:, :, 64 * half : 64 * half + 64, :].rearrange("p r s j -> p s r j")
-            src = k_raw[half][:].rearrange("p j (s r) -> p s r j", r=4)
-            nc.vector.tensor_copy(out=dst, in_=src)
+        def sigmoid(h, u0, u1):
+            nc.scalar.activation(out=sig[:, u0:u1, h, :], in_=og_sb[:, h, u0:u1, :], func=ACT.Sigmoid)
 
-        def interleave(eng_copy, dst, src):
-            eng_copy(
+        def sigmoid_couple(u):
+            g, c = divmod(u, 4)
+            src = og_sb[:, 2 * g : 2 * g + 2, c : c + 2, :].rearrange("m h c e -> m c h e")
+            nc.scalar.activation(out=sig[:, u : u + 2], in_=src, func=ACT.Sigmoid)
+
+        def interleave(dst, src):
+            nc.scalar.copy(
                 out=dst.rearrange("p (c i) j -> p c j i", i=4),
                 in_=src.rearrange("p j (c i) -> p c j i", i=4),
             )
 
-        def cast_q(u0):
-            interleave(nc.scalar.copy, q_bf[u0][:], q_raw[u0][:])
+        def round_q(u):
+            u0 = max(first for first in Q_LOADS if first <= u)
+            dealt = q_raw[u0][:].rearrange("p j (m c) -> p j c m", c=Q_LOADS[u0])
+            interleave(q_bf[u][:], dealt[:, :, u - u0, :])
 
-        def quant_q(u0):
-            cols = slice(128 * u0, 128 * (u0 + dict(q_spans)[u0]))
-            nc.vector.quantize_mx(
-                out=q_codes[:, cols].bitcast(FP8X4), scales=q_scales[:, cols], in_=q_bf[u0][:].rearrange("p q j -> p (q j)")
-            )
+        def round_k(half):
+            src = k_raw[half][:].rearrange("p j (s r) -> p s r j", r=PACK)
+            dst = k_bf[:, :, SH * half : SH * half + SH, :].rearrange("p r s j -> p s r j")
+            nc.vector.tensor_copy(out=dst[:, :, 0:2, :], in_=src[:, :, 0:2, :])
+            nc.scalar.copy(out=dst[:, :, 2:4, :], in_=src[:, :, 2:4, :])
+
+        def quantize(codes, scales, src):
+            nc.vector.quantize_mx(out=codes.bitcast(FP8X4), scales=scales, in_=src)
+
+        def quantize_k(half):
+            for r in range(PACK):
+                cols = slice(P * r + SH * half, P * r + SH * half + SH)
+                src = k_bf[:, r, SH * half : SH * half + SH, :].rearrange("p s j -> p (s j)")
+                quantize(k_codes[:, cols], k_scales[:, cols], src)
+
+        def quantize_q(u):
+            quantize(q_codes[u][:], q_scales[u][:], q_bf[u][:].rearrange("p m j -> p (m j)"))
+
+        def quantize_w(u, h0, h1):
+            cols = slice(QU * h0, QU * h1)
+            src = w_buf[u][:].bitcast(BF16)[:, QU * PACK * h0 : QU * PACK * h1]
+            quantize(w_codes[u][:, cols], w_scales[u][:, cols], src)
 
         def scores(u):
-            for r in range(4):
-                for hh in (1, 0):
-                    rows = slice(RT * hh, RT * hh + RT)
-                    cols = slice(128 * r, 128 * r + 128)
-                    nc.tensor.matmul_mx(
-                        out=s_ps[hh][u % 2][:, r, :],
-                        lhsT=k_codes[rows, cols].bitcast(FP8X4),
-                        lhsT_scale=k_scales[rows, cols],
-                        rhs=q_codes[rows, 128 * u : 128 * u + 128].bitcast(FP8X4),
-                        rhs_scale=q_scales[rows, 128 * u : 128 * u + 128],
-                        start=True,
-                        stop=True,
-                    )
-
-        def w_bf(u):
-            return w_buf[u][:].bitcast(BF16)
-
-        def weigh(u, hh):
-            dst = w_bf(u)[:, 512 * hh : 512 * hh + 512]
-            if hh in PAIRED:
-                nc.vector.tensor_tensor(
-                    out=dst.rearrange("p (c i r) -> p c r i", r=4, i=2),
-                    in0=s_ps[hh][u % 2][:].rearrange("p r (c i) -> p c r i", i=2),
-                    in1=t_pair[:],
-                    op=ALU.mult,
+            order = [(r, hh) for r in range(PACK) for hh in range(2)]
+            if u == 0:
+                order = sorted(order, key=lambda pair: pair[1])
+            for r, hh in order:
+                cols = slice(P * r, P * r + P)
+                nc.tensor.matmul_mx(
+                    out=s_ps[hh][u % 2][:, r, :],
+                    lhsT=k_codes[row_tile(hh), cols].bitcast(FP8X4),
+                    lhsT_scale=k_scales[row_tile(hh), cols],
+                    rhs=q_codes[u][row_tile(hh), :].bitcast(FP8X4),
+                    rhs_scale=q_scales[u][row_tile(hh), :],
+                    start=True,
+                    stop=True,
                 )
-            else:
+
+        def weigh(u):
+            for hh in range(2):
+                dst = w_buf[u][:].bitcast(BF16)[:, QU * PACK * hh : QU * PACK * (hh + 1)]
                 nc.vector.scalar_tensor_tensor(
-                    out=dst.rearrange("p (q r) -> p q r", r=4),
-                    in0=s_ps[hh][u % 2][:].rearrange("p r q -> p q r"),
+                    out=dst.rearrange("s (m r) -> s m r", r=PACK),
+                    in0=s_ps[hh][u % 2][:].rearrange("s r m -> s m r"),
                     scalar=0.0,
-                    in1=t_rep[:],
+                    in1=t_sb[:].unsqueeze(1).broadcast_to([P, QU, PACK]),
                     op0=ALU.max,
                     op1=ALU.mult,
                 )
 
-        def relu(u):
-            lo, hi = 512 * min(PAIRED), 512 * max(PAIRED) + 512
-            nc.vector.tensor_scalar(
-                out=w_bf(u)[:, lo:hi], in0=w_bf(u)[:, lo:hi], scalar1=0.0, scalar2=None, op0=ALU.max
-            )
-
-        def quant_w(u, h0, nh):
-            cols = slice(128 * h0, 128 * (h0 + nh))
-            nc.vector.quantize_mx(
-                out=w_codes[u][:, cols].bitcast(FP8X4),
-                scales=w_scales[u][:, cols],
-                in_=w_bf(u)[:, 512 * h0 : 512 * (h0 + nh)],
-            )
-
         def y_of(u, hh):
-            return y_ps[2 * (u % 2) + hh][:, u // 2, :]
+            pair, place = Y_PLACE[u]
+            return y_ps[2 * pair + hh][:, place, :]
 
         def values(u, hh):
-            cols = slice(128 * hh, 128 * hh + 128)
+            cols = slice(QU * hh, QU * hh + QU)
             nc.tensor.matmul_mx(
                 out=y_of(u, hh),
                 lhsT=w_codes[u][:, cols].bitcast(FP8X4),
@@ -172,152 +176,145 @@ def tile_rows_a_relu_onorm_gate_kernel(tc, qT, kT, t, v, gn, og, out):
                 stop=True,
             )
 
-        def sum_squares(u, hh):
-            n = 2 * u + hh
-            nc.scalar.activation(out=squares[hh][:], in_=y_of(u, hh), func=ACT.Square, accum_out=ssq[:, n : n + 1])
+        def sum_squares(u):
+            for hh in range(2):
+                n = 2 * u + hh
+                nc.scalar.activation(
+                    out=squares[hh][:], in_=y_of(u, hh), func=ACT.Square, accum_out=ssq[:, n : n + 1]
+                )
 
-        def inv_rms(n0, n1):
+        def inverse_norms(n0, n1):
             nc.scalar.activation(
-                out=rstd[:, n0:n1], in_=ssq[:, n0:n1], func=ACT.Abs_reciprocal_sqrt, scale=1.0 / E, bias=256.0 * 1e-5
+                out=inv_norm[:, n0:n1],
+                in_=ssq[:, n0:n1],
+                func=ACT.Abs_reciprocal_sqrt,
+                scale=1.0 / E,
+                bias=Y_DIV * Y_DIV * EPS,
             )
 
-        def gates(n0, n1, u):
-            cnt = n1 - n0
-            if GATE_ON_POOL:
-                dst = w_buf[u][:, 0 : cnt * E].rearrange("p (n e) -> p n e", e=E)
-                eng = nc.gpsimd
-            else:
-                dst = gate_own[:, n0:n1, :]
-                eng = nc.vector
+        def gates(u):
+            n0, n1 = GATE_BATCH[u]
+            dst = w_buf[u][:, 0 : (n1 - n0) * E].rearrange("m (n e) -> m n e", e=E)
             for n in range(n0, n1):
-                gate_at[n] = dst[:, n - n0, :]
-            eng.tensor_tensor(
-                out=dst, in0=sig_n[:, n0:n1, :], in1=gn_sb[:].unsqueeze(1).broadcast_to([P, cnt, E]), op=ALU.mult
+                gate_of[n] = dst[:, n - n0, :]
+            nc.gpsimd.tensor_tensor(
+                out=dst,
+                in0=sig[:].rearrange("m u h e -> m (u h) e")[:, n0:n1, :],
+                in1=gn_sb[:].unsqueeze(1).broadcast_to([P, n1 - n0, E]),
+                op=ALU.mult,
             )
 
         def finish(u, hh):
             n = 2 * u + hh
             nc.vector.scalar_tensor_tensor(
-                out=res[u][:, hh, :],
+                out=res[u // 2][:, hh, u % 2, :],
                 in0=y_of(u, hh),
-                scalar=rstd[:, n : n + 1],
-                in1=gate_at[n],
+                scalar=inv_norm[:, n : n + 1],
+                in1=gate_of[n],
                 op0=ALU.mult,
                 op1=ALU.mult,
             )
 
-        def store(u, h0, nh):
-            g, c = divmod(u, 4)
-            dst = out[2 * g + h0 : 2 * g + h0 + nh, 128 * c : 128 * c + 128, :].rearrange("h p e -> p h e")
-            nc.sync.dma_start(out=dst, in_=res[u][:, h0 : h0 + nh, :])
+        def store(u, h0, h1):
+            if u < 2:
+                dst = out[0:2, QU * u : QU * u + QU, :].rearrange("h m e -> m h e")
+            else:
+                dst = couple_rows(out, u - u % 2)[:, :, E * (u % 2) : E * (u % 2) + E]
+            nc.sync.dma_start(out=dst[:, h0:h1, :], in_=res[u // 2][:, h0:h1, u % 2, :])
 
-        k_src = kT[0].rearrange("(p j) n -> p j n", j=4)
-        nc.scalar.dma_start(out=t_sb[:], in_=t.rearrange("(p j) o -> p (j o)", j=4))
-        load_og(nc.scalar, 0, 1, 0, 1)
+        def finish_and_store(u):
+            finish(u, 0)
+            finish(u, 1)
+            store(u, 0, 2)
+
+        load_og(nc.scalar, 0, 0, 1)
+        for hh, eng in enumerate(queue_of_row_tile):
+            src = qT[hh].rearrange("(p j) q -> p j q", j=PACK)
+            eng.dma_start(out=q_raw[0][row_tile(hh)], in_=src[:, :, 0:QU])
+        k_src = kT[0].rearrange("(p j) i -> p j i", j=PACK)
         for half in range(2):
-            cols = slice(256 * half, 256 * half + 256)
-            nc.sync.dma_start(out=k_raw[half][0:RT], in_=k_src[:, :, cols])
-            nc.scalar.dma_start(out=k_raw[half][RT:P], in_=k_src[:, :, cols])
-        load_q(0, 1)
-        load_q(1, 1)
-        load_q(2, 2)
-        nc.sync.dma_start(out=v_raw[:], in_=v[0].rearrange("(p j) e -> p j e", j=4))
+            for hh, eng in enumerate(queue_of_row_tile):
+                eng.dma_start(out=k_raw[half][row_tile(hh)], in_=k_src[:, :, HALF * half : HALF * half + HALF])
+        nc.sync.dma_start(out=t_sb[:], in_=t.rearrange("(s r) o -> s (r o)", r=PACK))
+        load_q(1)
+        load_q(2)
+        nc.sync.dma_start(out=v_raw[:], in_=v[0].rearrange("(s r) e -> s r e", r=PACK))
+        load_og(nc.sync, 1, 0, 2)
+        load_og(nc.sync, 0, 1, 2)
         nc.sync.dma_start(out=gn_sb[:], in_=gn)
-        load_og(nc.sync, 0, 1, 1, 3)
-        load_og(nc.sync, 1, 1, 0, 4)
-        load_q(4, 2)
-        load_og(nc.sync, 2, 2, 0, 4)
-        load_q(6, 2)
+        load_q(4)
+        for u in (2, 4, 6):
+            load_og_couple(u)
+        load_q(6)
 
         sigmoid(0, 0, 1)
-        nc.gpsimd.tensor_scalar(out=t_two[:], in0=t_sb[:], scalar1=0.0, scalar2=2.0, op0=ALU.is_ge, op1=ALU.mult)
-        nc.gpsimd.tensor_scalar(out=t_sign[:], in0=t_two[:], scalar1=1.0, scalar2=-1.0, op0=ALU.mult, op1=ALU.add)
-        nc.scalar.activation(
-            out=t_pair[:], in_=t_sb[:].unsqueeze(1).unsqueeze(3).broadcast_to([P, 64, 4, 2]), func=ACT.Abs
-        )
-        nc.scalar.activation(out=t_rep[:], in_=t_sb[:].unsqueeze(1).broadcast_to([P, 128, 4]), func=ACT.Abs)
-        cast_k(0)
-        cast_k(1)
-        cast_q(0)
-        for rr in range(2):
-            cols = slice(256 * rr, 256 * rr + 256)
-            nc.vector.quantize_mx(
-                out=k_codes[:, cols].bitcast(FP8X4),
-                scales=k_scales[:, cols],
-                in_=k_bf[:, 2 * rr : 2 * rr + 2].rearrange("p r s j -> p (r s j)"),
-            )
-        quant_q(0)
+        round_q(0)
+        round_k(0)
+        quantize_q(0)
+        quantize_k(0)
+        round_k(1)
+        quantize_k(1)
         scores(0)
-        cast_q(1)
-        quant_q(1)
+        round_q(1)
+        quantize_q(1)
         scores(1)
-        cast_q(2)
-        for j in range(4):
-            nc.scalar.activation(out=v_sgn[:, j, :], in_=v_raw[:, j, :], func=ACT.Copy, scale=t_sign[:, j : j + 1])
-        interleave(nc.scalar.copy, v_bf[:], v_sgn[:])
-        sigmoid(0, 1, 3)
-        sigmoid(1, 0, 4)
+        round_q(2)
+        round_q(3)
+        interleave(v_bf[:], v_raw[:])
+        sigmoid(1, 0, 2)
+        sigmoid(0, 1, 2)
 
-        for u in range(UNITS):
-            last = u == UNITS - 1
-            weigh(u, 1)
-            weigh(u, 0)
-            if last:
-                relu(u)
-                quant_w(u, 0, 1)
-                values(u, 0)
-                sum_squares(u, 0)
-                inv_rms(2 * u, 2 * u + 1)
-                quant_w(u, 1, 1)
-                values(u, 1)
-                sum_squares(u, 1)
-                inv_rms(2 * u + 1, 2 * u + 2)
-            for f in FINISH.get(u, []):
-                finish(f, 0)
-                finish(f, 1)
-                store(f, 0, 2)
-            if last:
-                break
-            relu(u)
+        last = UNITS - 1
+        for u in range(last):
+            ahead = u + 2
+            weigh(u)
+            for f in FINISH_IN_STEP.get(u, []):
+                finish_and_store(f)
+            if u in SQUARES_IN_STEP:
+                units, tiles = SQUARES_IN_STEP[u]
+                for f in units:
+                    sum_squares(f)
+                inverse_norms(*tiles)
             if u == 1:
-                nc.vector.quantize_mx(
-                    out=v_codes[:].bitcast(FP8X4), scales=v_scales[:], in_=v_bf[:].rearrange("p e j -> p (e j)")
-                )
-                values(0, 0)
-                values(0, 1)
-            if u + 2 < UNITS:
-                if u % 2 == 0:
-                    quant_q(u + 2)
-                scores(u + 2)
-            quant_w(u, 0, 1)
-            quant_w(u, 1, 1)
-            if u >= 1:
-                values(u, 0)
-                values(u, 1)
-            if u == 0:
-                cast_q(4)
+                quantize(v_codes[:], v_scales[:], v_bf[:].rearrange("s e r -> s (e r)"))
+            if ahead < UNITS:
+                quantize_q(ahead)
+            if ahead < UNITS and u != 1:
+                scores(ahead)
+            quantize_w(u, 0, 2)
+            for f in {0: [], 1: [0, 1]}.get(u, [u]):
+                values(f, 0)
+                values(f, 1)
             if u == 1:
-                sigmoid(2, 0, 4)
-                sigmoid(3, 0, 4)
-                sum_squares(0, 0)
-                sum_squares(0, 1)
-                inv_rms(0, 2)
-            if u == 2:
-                cast_q(6)
-                for f in (1, 2):
-                    sum_squares(f, 0)
-                    sum_squares(f, 1)
-                    inv_rms(2 * f, 2 * f + 2)
-            if u >= 3:
-                sum_squares(u, 0)
-                sum_squares(u, 1)
-                inv_rms(2 * u, 2 * u + 2)
-            if u in WINDOW:
-                gates(WINDOW[u][0], WINDOW[u][1], u)
-        for f in FINISH[UNITS]:
+                scores(ahead)
+            gates(u)
+            if u == 1:
+                round_q(4)
+                round_q(5)
+                sigmoid_couple(2)
+                sum_squares(0)
+                sigmoid_couple(4)
+                sigmoid_couple(6)
+                sum_squares(1)
+                round_q(6)
+                inverse_norms(0, 4)
+                round_q(7)
+        sum_squares(last - 1)
+        inverse_norms(2 * last - 2, 2 * last)
+
+        weigh(last)
+        for hh in range(2):
+            quantize_w(last, hh, hh + 1)
+            values(last, hh)
+            finish(2, hh)
+        store(2, 0, 2)
+        sum_squares(last)
+        inverse_norms(2 * last, 2 * last + 2)
+        for f in (4, 5):
             finish(f, 0)
             finish(f, 1)
-            store(f, 0, 2)
+        nc.sync.dma_start(out=couple_rows(out, 4), in_=res[2][:].rearrange("m h c e -> m h (c e)"))
+        finish_and_store(6)
         for hh in range(2):
-            finish(UNITS - 1, hh)
-            store(UNITS - 1, hh, 1)
+            finish(last, hh)
+            store(last, hh, hh + 1)

from contextlib import ExitStack

import concourse.mybir as mybir

H, D, NQ, N, E = 4, 256, 512, 512, 128
FLOPS = 2 * H * N * NQ * D + 2 * H * NQ * N * E

F32 = mybir.dt.float32
BF16 = mybir.dt.bfloat16
U32 = mybir.dt.uint32
U8 = mybir.dt.uint8
FP8X4 = mybir.dt.float8_e4m3fn_x4
ACT = mybir.ActivationFunctionType
ALU = mybir.AluOpType

P = 128
PACK = 4
ROWS = D // PACK
QU = 128
UNITS = H // 2 * NQ // QU
HALF = N // 2
SH = HALF // PACK
EPS = 1e-5
Y_DIV = 16.0

Q_LOADS = {0: 1, 1: 1, 2: 2, 4: 2, 6: 2}
Y_PLACE = [(1, 0), (1, 1), (0, 0), (1, 2), (0, 1), (0, 2), (0, 3), (1, 3)]
GATE_BATCH = [(0, 1), (1, 3), (3, 5), (5, 7), (7, 11), (11, 14), (14, 16)]
FINISH_IN_STEP = {5: [0, 1], 6: [3]}
SQUARES_IN_STEP = {5: ([2, 4, 3], (4, 10)), 6: ([5], (10, 12))}


def tile_rows_a_relu_onorm_gate_kernel(tc, qT, kT, t, v, gn, og, out):
    nc = tc.nc
    with ExitStack() as ctx:
        sb = ctx.enter_context(tc.tile_pool(name="sb", bufs=1))
        ps = ctx.enter_context(tc.psum_pool(name="ps", bufs=1))
        ctx.enter_context(tc.manual_schedule())

        def sbuf(name, shape, dtype):
            return sb.tile([P] + shape, dtype, name=name, align_bytes=64)

        k_raw = [sbuf("k_raw%d" % half, [PACK, HALF], F32) for half in range(2)]
        k_bf = sbuf("k_bf", [PACK, P, PACK], BF16)
        k_codes = sbuf("k_codes", [N], U32)
        k_scales = sbuf("k_scales", [N], U8)
        q_raw = {u0: sbuf("q_raw%d" % u0, [PACK, QU * n], F32) for u0, n in Q_LOADS.items()}
        q_bf = [sbuf("q_bf%d" % u, [QU, PACK], BF16) for u in range(UNITS)]
        q_codes = [sbuf("q_codes%d" % u, [QU], U32) for u in range(UNITS)]
        q_scales = [sbuf("q_scales%d" % u, [QU], U8) for u in range(UNITS)]
        v_raw = sbuf("v_raw", [PACK, E], F32)
        v_bf = sbuf("v_bf", [E, PACK], BF16)
        v_codes = sbuf("v_codes", [E], U32)
        v_scales = sbuf("v_scales", [E], U8)
        t_sb = sbuf("t_sb", [PACK], F32)
        gn_sb = sbuf("gn_sb", [E], F32)
        og_sb = sbuf("og_sb", [H, UNITS // 2, E], F32)
        sig = sbuf("sig", [UNITS, 2, E], F32)
        w_buf = [sbuf("w_buf%d" % u, [QU * PACK], F32) for u in range(UNITS)]
        w_codes = [sbuf("w_codes%d" % u, [2 * QU], U32) for u in range(UNITS)]
        w_scales = [sbuf("w_scales%d" % u, [2 * QU], U8) for u in range(UNITS)]
        squares = [sbuf("squares%d" % hh, [E], BF16) for hh in range(2)]
        ssq = sbuf("ssq", [2 * UNITS], F32)
        inv_norm = sbuf("inv_norm", [2 * UNITS], F32)
        res = [sbuf("res%d" % c, [2, 2, E], F32) for c in range(UNITS // 2)]
        s_ps = [[ps.tile([P, PACK, QU], F32, name="s_ps%d%d" % (hh, i)) for i in range(2)] for hh in range(2)]
        y_ps = [ps.tile([P, 4, E], F32, name="y_ps%d" % i) for i in range(4)]
        gate_of = {}
        queue_of_row_tile = (nc.sync, nc.scalar)

        def row_tile(hh):
            return slice(ROWS * hh, ROWS * hh + ROWS)

        def couple_rows(dram, u):
            g, c = divmod(u, 4)
            rows = dram[2 * g : 2 * g + 2, QU * c : QU * (c + 2), :]
            return rows.rearrange("h (m c) e -> m h (c e)", c=2)

        def load_q(u0):
            g, c = divmod(u0, 4)
            src = qT[2 * g : 2 * g + 2].rearrange("h (p j) q -> (h p) j q", j=PACK)
            nc.sync.dma_start(out=q_raw[u0][:], in_=src[:, :, QU * c : QU * (c + Q_LOADS[u0])])

        def load_og(eng, h, u0, u1):
            src = og[h].rearrange("(c m) e -> m c e", m=P)
            eng.dma_start(out=og_sb[:, h, u0:u1, :], in_=src[:, u0:u1, :])

        def load_og_couple(u):
            g, c = divmod(u, 4)
            dst = og_sb[:, 2 * g : 2 * g + 2, c : c + 2, :].rearrange("m h c e -> m h (c e)")
            nc.sync.dma_start(out=dst, in_=couple_rows(og, u))

        def sigmoid(h, u0, u1):
            nc.scalar.activation(out=sig[:, u0:u1, h, :], in_=og_sb[:, h, u0:u1, :], func=ACT.Sigmoid)

        def sigmoid_couple(u):
            g, c = divmod(u, 4)
            src = og_sb[:, 2 * g : 2 * g + 2, c : c + 2, :].rearrange("m h c e -> m c h e")
            nc.scalar.activation(out=sig[:, u : u + 2], in_=src, func=ACT.Sigmoid)

        def interleave(dst, src):
            nc.scalar.copy(
                out=dst.rearrange("p (c i) j -> p c j i", i=4),
                in_=src.rearrange("p j (c i) -> p c j i", i=4),
            )

        def round_q(u):
            u0 = max(first for first in Q_LOADS if first <= u)
            dealt = q_raw[u0][:].rearrange("p j (m c) -> p j c m", c=Q_LOADS[u0])
            interleave(q_bf[u][:], dealt[:, :, u - u0, :])

        def round_k(half):
            src = k_raw[half][:].rearrange("p j (s r) -> p s r j", r=PACK)
            dst = k_bf[:, :, SH * half : SH * half + SH, :].rearrange("p r s j -> p s r j")
            nc.vector.tensor_copy(out=dst[:, :, 0:2, :], in_=src[:, :, 0:2, :])
            nc.scalar.copy(out=dst[:, :, 2:4, :], in_=src[:, :, 2:4, :])

        def quantize(codes, scales, src):
            nc.vector.quantize_mx(out=codes.bitcast(FP8X4), scales=scales, in_=src)

        def quantize_k(half):
            for r in range(PACK):
                cols = slice(P * r + SH * half, P * r + SH * half + SH)
                src = k_bf[:, r, SH * half : SH * half + SH, :].rearrange("p s j -> p (s j)")
                quantize(k_codes[:, cols], k_scales[:, cols], src)

        def quantize_q(u):
            quantize(q_codes[u][:], q_scales[u][:], q_bf[u][:].rearrange("p m j -> p (m j)"))

        def quantize_w(u, h0, h1):
            cols = slice(QU * h0, QU * h1)
            src = w_buf[u][:].bitcast(BF16)[:, QU * PACK * h0 : QU * PACK * h1]
            quantize(w_codes[u][:, cols], w_scales[u][:, cols], src)

        def scores(u):
            order = [(r, hh) for r in range(PACK) for hh in range(2)]
            if u == 0:
                order = sorted(order, key=lambda pair: pair[1])
            for r, hh in order:
                cols = slice(P * r, P * r + P)
                nc.tensor.matmul_mx(
                    out=s_ps[hh][u % 2][:, r, :],
                    lhsT=k_codes[row_tile(hh), cols].bitcast(FP8X4),
                    lhsT_scale=k_scales[row_tile(hh), cols],
                    rhs=q_codes[u][row_tile(hh), :].bitcast(FP8X4),
                    rhs_scale=q_scales[u][row_tile(hh), :],
                    start=True,
                    stop=True,
                )

        def weigh(u):
            for hh in range(2):
                dst = w_buf[u][:].bitcast(BF16)[:, QU * PACK * hh : QU * PACK * (hh + 1)]
                nc.vector.scalar_tensor_tensor(
                    out=dst.rearrange("s (m r) -> s m r", r=PACK),
                    in0=s_ps[hh][u % 2][:].rearrange("s r m -> s m r"),
                    scalar=0.0,
                    in1=t_sb[:].unsqueeze(1).broadcast_to([P, QU, PACK]),
                    op0=ALU.max,
                    op1=ALU.mult,
                )

        def y_of(u, hh):
            pair, place = Y_PLACE[u]
            return y_ps[2 * pair + hh][:, place, :]

        def values(u, hh):
            cols = slice(QU * hh, QU * hh + QU)
            nc.tensor.matmul_mx(
                out=y_of(u, hh),
                lhsT=w_codes[u][:, cols].bitcast(FP8X4),
                lhsT_scale=w_scales[u][:, cols],
                rhs=v_codes[:].bitcast(FP8X4),
                rhs_scale=v_scales[:],
                start=True,
                stop=True,
            )

        def sum_squares(u):
            for hh in range(2):
                n = 2 * u + hh
                nc.scalar.activation(
                    out=squares[hh][:], in_=y_of(u, hh), func=ACT.Square, accum_out=ssq[:, n : n + 1]
                )

        def inverse_norms(n0, n1):
            nc.scalar.activation(
                out=inv_norm[:, n0:n1],
                in_=ssq[:, n0:n1],
                func=ACT.Abs_reciprocal_sqrt,
                scale=1.0 / E,
                bias=Y_DIV * Y_DIV * EPS,
            )

        def gates(u):
            n0, n1 = GATE_BATCH[u]
            dst = w_buf[u][:, 0 : (n1 - n0) * E].rearrange("m (n e) -> m n e", e=E)
            for n in range(n0, n1):
                gate_of[n] = dst[:, n - n0, :]
            nc.gpsimd.tensor_tensor(
                out=dst,
                in0=sig[:].rearrange("m u h e -> m (u h) e")[:, n0:n1, :],
                in1=gn_sb[:].unsqueeze(1).broadcast_to([P, n1 - n0, E]),
                op=ALU.mult,
            )

        def finish(u, hh):
            n = 2 * u + hh
            nc.vector.scalar_tensor_tensor(
                out=res[u // 2][:, hh, u % 2, :],
                in0=y_of(u, hh),
                scalar=inv_norm[:, n : n + 1],
                in1=gate_of[n],
                op0=ALU.mult,
                op1=ALU.mult,
            )

        def store(u, h0, h1):
            if u < 2:
                dst = out[0:2, QU * u : QU * u + QU, :].rearrange("h m e -> m h e")
            else:
                dst = couple_rows(out, u - u % 2)[:, :, E * (u % 2) : E * (u % 2) + E]
            nc.sync.dma_start(out=dst[:, h0:h1, :], in_=res[u // 2][:, h0:h1, u % 2, :])

        def finish_and_store(u):
            finish(u, 0)
            finish(u, 1)
            store(u, 0, 2)

        load_og(nc.scalar, 0, 0, 1)
        for hh, eng in enumerate(queue_of_row_tile):
            src = qT[hh].rearrange("(p j) q -> p j q", j=PACK)
            eng.dma_start(out=q_raw[0][row_tile(hh)], in_=src[:, :, 0:QU])
        k_src = kT[0].rearrange("(p j) i -> p j i", j=PACK)
        for half in range(2):
            for hh, eng in enumerate(queue_of_row_tile):
                eng.dma_start(out=k_raw[half][row_tile(hh)], in_=k_src[:, :, HALF * half : HALF * half + HALF])
        nc.sync.dma_start(out=t_sb[:], in_=t.rearrange("(s r) o -> s (r o)", r=PACK))
        load_q(1)
        load_q(2)
        nc.sync.dma_start(out=v_raw[:], in_=v[0].rearrange("(s r) e -> s r e", r=PACK))
        load_og(nc.sync, 1, 0, 2)
        load_og(nc.sync, 0, 1, 2)
        nc.sync.dma_start(out=gn_sb[:], in_=gn)
        load_q(4)
        for u in (2, 4, 6):
            load_og_couple(u)
        load_q(6)

        sigmoid(0, 0, 1)
        round_q(0)
        round_k(0)
        quantize_q(0)
        quantize_k(0)
        round_k(1)
        quantize_k(1)
        scores(0)
        round_q(1)
        quantize_q(1)
        scores(1)
        round_q(2)
        round_q(3)
        interleave(v_bf[:], v_raw[:])
        sigmoid(1, 0, 2)
        sigmoid(0, 1, 2)

        last = UNITS - 1
        for u in range(last):
            ahead = u + 2
            weigh(u)
            for f in FINISH_IN_STEP.get(u, []):
                finish_and_store(f)
            if u in SQUARES_IN_STEP:
                units, tiles = SQUARES_IN_STEP[u]
                for f in units:
                    sum_squares(f)
                inverse_norms(*tiles)
            if u == 1:
                quantize(v_codes[:], v_scales[:], v_bf[:].rearrange("s e r -> s (e r)"))
            if ahead < UNITS:
                quantize_q(ahead)
            if ahead < UNITS and u != 1:
                scores(ahead)
            quantize_w(u, 0, 2)
            for f in {0: [], 1: [0, 1]}.get(u, [u]):
                values(f, 0)
                values(f, 1)
            if u == 1:
                scores(ahead)
            gates(u)
            if u == 1:
                round_q(4)
                round_q(5)
                sigmoid_couple(2)
                sum_squares(0)
                sigmoid_couple(4)
                sigmoid_couple(6)
                sum_squares(1)
                round_q(6)
                inverse_norms(0, 4)
                round_q(7)
        sum_squares(last - 1)
        inverse_norms(2 * last - 2, 2 * last)

        weigh(last)
        for hh in range(2):
            quantize_w(last, hh, hh + 1)
            values(last, hh)
            finish(2, hh)
        store(2, 0, 2)
        sum_squares(last)
        inverse_norms(2 * last, 2 * last + 2)
        for f in (4, 5):
            finish(f, 0)
            finish(f, 1)
        nc.sync.dma_start(out=couple_rows(out, 4), in_=res[2][:].rearrange("m h c e -> m h (c e)"))
        finish_and_store(6)
        for hh in range(2):
            finish(last, hh)
            store(last, hh, hh + 1)
